import numpy as np
import ml_dtypes


def mxq(x, axis, fmt="e4m3"):
    dtype, down = {"e4m3": (ml_dtypes.float8_e4m3fn, 7), "e5m2": (ml_dtypes.float8_e5m2, 14)}[fmt]
    v = np.moveaxis(np.asarray(x, np.float32).astype(ml_dtypes.bfloat16).astype(np.float64), axis, -1)
    blocks = v.reshape(v.shape[:-1] + (-1, 32))
    amax = np.abs(blocks).max(-1, keepdims=True)
    byte = np.maximum(np.where(amax > 0, np.frexp(amax)[1] - 1 + 127, 0) - down, 1)
    scale = np.exp2(byte - 127.0)
    codes = (blocks / scale).astype(np.float32).astype(dtype).astype(np.float64)
    return np.moveaxis((codes * scale).reshape(v.shape), -1, axis)


WIDE = False


def mx_kscale(k):
    if not WIDE:
        return np.ones(k)
    levels = np.array([10, -10, 5, -5, 0])
    if k % 512:
        return np.exp2(np.random.permutation(np.resize(levels, k // 32))).repeat(32)
    a = np.empty((k // 512, 16))
    for p in range(k // 512):
        a[p, :8] = np.random.permutation(np.resize(levels, 8))
        for g in range(8):
            far = levels[np.abs(levels - a[p, g]) >= 10]
            a[p, g + 8] = far[np.random.randint(len(far))]
    return np.exp2(a.ravel()).repeat(32)


def f64(x):
    return np.asarray(x).astype(np.float64)


def striped(idx):
    return np.tile(idx.reshape(-1, 16).T, (8, 1)).astype(np.uint16)


def unstriped(offs):
    return offs[:16].T.reshape(-1).astype(np.int64)


def striped8(idx):
    return np.concatenate([x.reshape(-1, 16).T for x in idx]).astype(np.uint16)


def runs(offs, k):
    lists = np.stack([offs[16 * r : 16 * r + 16].T.reshape(-1) for r in range(8)]).astype(np.int64)
    return lists[np.arange(k) % 512 // 64]


def pack_weight(w):
    k, n = w.shape
    w = f64(np.asarray(w, np.float32).astype(ml_dtypes.bfloat16)).reshape(k // 32, 32, n)
    amax = np.abs(w).max(1)
    byte = np.clip(np.where(amax > 0, np.frexp(amax)[1] - 1 + 127 - 7, 1), 1, 254)
    scaled = (w * np.exp2(127.0 - byte)[:, None, :]).reshape(k, n).astype(np.float32)
    words = np.ascontiguousarray(scaled.reshape(k // 512, 128, 4, n).transpose(0, 1, 3, 2)).astype(ml_dtypes.float8_e4m3fn).view(np.uint8)
    return words, np.ascontiguousarray(byte.astype(np.uint8).reshape(k // 512, 16, n))


def unpack_weight(words, scales):
    g, p, n, _ = words.shape
    vals = np.ascontiguousarray(words).view(ml_dtypes.float8_e4m3fn).astype(np.float64) * np.repeat(np.exp2(scales.astype(np.float64) - 127.0), 8, axis=1)[..., None]
    return vals.transpose(0, 1, 3, 2).reshape(g * 512, n)


K, T, S, N, H = 512, 2048, 512, 512, 512


def setup_inputs():
    n = np.random.standard_normal
    s = mx_kscale(K)[:, None]
    u = mx_kscale(H)
    packed_xT = pack_weight(n((K, T)) * s)
    return {
        "x_words": packed_xT[0],
        "x_scales": packed_xT[1],
        "w1": (n((K, H)) / np.sqrt(K) / s).astype(np.float32),
        "w2": (n((K, H)) / np.sqrt(K) / s).astype(np.float32),
        "w3": (n((K, H)) / np.sqrt(K) / s).astype(np.float32),
        "gn": (np.random.uniform(0.5, 1.5, (H, 1)) * u[:, None]).astype(np.float32),
        "w4": (n((H, N)) / np.sqrt(H) / u[:, None]).astype(np.float32),
        "offs": striped(np.random.permutation(T)[:S]),
        "two": striped(np.random.permutation(T)[:S]),
        "three": striped(np.random.permutation(T)[:S]),
        "n1": striped8(np.stack([np.random.permutation(S) for _ in range(8)])),
        "n2": striped8(np.stack([np.random.permutation(S) for _ in range(8)])),
        "n3": striped8(np.stack([np.random.permutation(S) for _ in range(8)])),
        "n4": striped8(np.stack([np.random.permutation(S) for _ in range(8)])),
        "n5": striped8(np.stack([np.random.permutation(S) for _ in range(8)])),
    }


def reference(x_words, x_scales, w1, w2, w3, gn, w4, offs, two, three, n1, n2, n3, n4, n5):
    xq = unpack_weight(x_words, x_scales)[:, unstriped(offs)]
    y = mxq(f64(w1), 0, "e4m3").T @ xq
    x_two = unpack_weight(x_words, x_scales)[:, unstriped(two)]
    d = mxq(f64(w2), 0, "e4m3").T @ x_two
    m1 = np.maximum(y, d[np.arange(H)[:, None], runs(n2, H)]) - (np.minimum(y[np.arange(H)[:, None], runs(n1, H)], d))
    x_three = unpack_weight(x_words, x_scales)[:, unstriped(three)]
    b = mxq(f64(w3), 0, "e4m3").T @ x_three
    z = f64(gn) * (m1 * (np.tanh(b[np.arange(H)[:, None], runs(n3, H)] - (b[np.arange(H)[:, None], runs(n4, H)]))))
    h = mxq(f64(w4), 0, "e4m3").T @ mxq(z, 0, "e4m3")
    return np.maximum(h, h[np.arange(N)[:, None], runs(n5, N)])

@@ -1,0 +1,249 @@
+from contextlib import ExitStack
+
+import concourse.mybir as mybir
+from concourse.masks import make_identity
+
+F32 = mybir.dt.float32
+BF16 = mybir.dt.bfloat16
+I32 = mybir.dt.int32
+U32 = mybir.dt.uint32
+U16 = mybir.dt.uint16
+U8 = mybir.dt.uint8
+FP8X4 = mybir.dt.float8_e4m3fn_x4
+ACT = mybir.ActivationFunctionType
+ALU = mybir.AluOpType
+
+P = 128
+PACK = 4
+T_COLS = 2048
+S = 512
+HALF = 256
+FLOPS = 4 * 2 * 512 * 512 * 512
+
+MIX_PIECES = ((0, 256), (256, 384), (384, 512))
+
+
+def tile_picked_triomaxbjointbbig_none_p_kernel(
+    tc, x_words, x_scales, w1, w2, w3, gn, w4, offs, two, three, n1, n2, n3, n4, n5, out
+):
+    nc = tc.nc
+    with ExitStack() as ctx:
+        lists = ctx.enter_context(tc.tile_pool(name="lists", bufs=1))
+        sb = ctx.enter_context(tc.tile_pool(name="sb", bufs=1))
+        ps = ctx.enter_context(tc.psum_pool(name="ps", bufs=1))
+
+        def load_list(src, name):
+            tile = lists.tile([P, S // 16], U16, name=name)
+            nc.sync.dma_start(out=tile[:], in_=src)
+            return tile
+
+        def load_weight(src, name):
+            raw = sb.tile([P, PACK, S], F32, name=name)
+            nc.sync.dma_start(out=raw[:], in_=src.rearrange("(p j) c -> p j c", j=PACK))
+            return raw
+
+        def entries(tile, lo, hi):
+            return tile[:, lo // 16 : hi // 16]
+
+        l_three = load_list(three, "l_three")
+        x_bytes = sb.tile([P, T_COLS], U8, name="x_bytes")
+        for q in range(4):
+            nc.sync.dma_start(
+                out=x_bytes[32 * q : 32 * q + 32, :].bitcast(I32),
+                in_=x_scales[0, 4 * q : 4 * q + 4, :].bitcast(I32).partition_broadcast(8),
+            )
+        l_offs = load_list(offs, "l_offs")
+        l_two = load_list(two, "l_two")
+        raw3 = load_weight(w3, "raw3")
+        x_codes = sb.tile([P, T_COLS], U32, name="x_codes")
+        nc.sync.dma_start(
+            out=x_codes[:].bitcast(I32), in_=x_words[0].rearrange("p n t -> p (n t)").bitcast(I32)
+        )
+        gain = sb.tile([P, PACK], F32, name="gain")
+        nc.sync.dma_start(out=gain[:], in_=gn.rearrange("(p t) o -> p (t o)", t=PACK))
+        l_n4 = load_list(n4, "l_n4")
+        l_n3 = load_list(n3, "l_n3")
+        raw1 = load_weight(w1, "raw1")
+        raw2 = load_weight(w2, "raw2")
+        l_n2 = load_list(n2, "l_n2")
+        l_n1 = load_list(n1, "l_n1")
+        raw4 = load_weight(w4, "raw4")
+        l_n5 = load_list(n5, "l_n5")
+
+        ident = sb.tile([P, P], F32, name="ident")
+        make_identity(nc, ident[:])
+        warm = sb.tile([P, 1], F32, name="warm")
+        nc.scalar.activation(out=warm[:], in_=ident[:, 0:1], func=ACT.Tanh)
+
+        def round_weight(raw, tag):
+            rounded = sb.tile([P, PACK * S], BF16, name=tag, tag=tag, align_bytes=64)
+            nc.scalar.copy(
+                out=rounded[:].rearrange("p (t m j) -> p m j t", t=PACK, j=PACK),
+                in_=raw[:].rearrange("p j (m t) -> p m j t", t=PACK),
+            )
+            return rounded
+
+        def quantize(rounded, width, name):
+            codes = sb.tile([P, width], U32, name=name + "_codes", align_bytes=64)
+            scales = sb.tile([P, width], U8, name=name + "_scales", align_bytes=64)
+            nc.vector.quantize_mx(out=codes[:].bitcast(FP8X4), scales=scales[:], in_=rounded)
+            return codes, scales
+
+        def pick(window, lst, dtype, name, tag=""):
+            picked = sb.tile([P, S], dtype, name=name, tag=tag or name, align_bytes=64)
+            nc.vector.tensor_copy(out=picked[:], in_=window[:].indirect(lst[:]))
+            return picked
+
+        def product(acc, weight, t, moving):
+            cols = slice(t * P, (t + 1) * P)
+            nc.tensor.matmul_mx(
+                out=acc,
+                lhsT=weight[0][:, cols].bitcast(FP8X4),
+                lhsT_scale=weight[1][:, cols],
+                rhs=moving[0][:].bitcast(FP8X4),
+                rhs_scale=moving[1][:],
+                start=True,
+                stop=True,
+            )
+
+        def project(weight, tokens, t, factor, name):
+            acc = ps.tile([P, S], F32, name="acc", tag="acc", bufs=2)
+            product(acc[:], weight, t, tokens)
+            row = sb.tile([P, S], F32, name=name)
+            nc.scalar.activation(out=row[:], in_=acc[:], func=ACT.Copy, scale=factor[:, t : t + 1])
+            return row
+
+        bytes3 = pick(x_bytes, l_three, U8, "bytes3")
+        bytes1 = pick(x_bytes, l_offs, U8, "bytes1")
+        bytes2 = pick(x_bytes, l_two, U8, "bytes2")
+        rounded3 = round_weight(raw3, "rounded3")
+        codes3 = pick(x_codes, l_three, U32, "codes3")
+        q3 = quantize(rounded3[:], S, "q3")
+        codes1 = pick(x_codes, l_offs, U32, "codes1", "rounded3")
+        codes2 = pick(x_codes, l_two, U32, "codes2")
+
+        g_sign = sb.tile([P, PACK], F32, name="g_sign")
+        g_abs = sb.tile([P, PACK], F32, name="g_abs")
+        g_neg = sb.tile([P, PACK], F32, name="g_neg")
+        nc.scalar.activation(out=g_sign[:], in_=gain[:], func=ACT.Sign)
+        nc.scalar.activation(out=g_abs[:], in_=gain[:], func=ACT.Abs)
+        nc.scalar.activation(out=g_neg[:], in_=g_abs[:], func=ACT.Copy, scale=-1.0)
+
+        b_rows = [project(q3, (codes3, bytes3), t, g_sign, "b%d" % t) for t in range(PACK)]
+        rounded1 = round_weight(raw1, "rounded1")
+        rounded2 = round_weight(raw2, "rounded2")
+        q1 = quantize(rounded1[:], S, "q1")
+        q2 = quantize(rounded2[:], S, "q2")
+        y_rows, nd_rows = [], []
+        for t in range(PACK):
+            y_rows.append(project(q1, (codes1, bytes1), t, g_abs, "y%d" % t))
+            nd_rows.append(project(q2, (codes2, bytes2), t, g_neg, "nd%d" % t))
+
+        b4 = {}
+        for t in range(PACK):
+            for h in range(2):
+                tag = "rounded1" if (t, h) == (3, 0) else "b4_%d_%d" % (t, h)
+                b4[t, h] = sb.tile([P, HALF], F32, name="b4_%d_%d" % (t, h), tag=tag, align_bytes=64)
+                nc.vector.tensor_copy(
+                    out=b4[t, h][:], in_=b_rows[t][:].indirect(entries(l_n4, h * HALF, (h + 1) * HALF))
+                )
+        diff = {}
+        for h in range(2):
+            for t in range(PACK):
+                tag = "rounded2" if (t, h) == (3, 0) else "diff_%d_%d" % (t, h)
+                diff[t, h] = sb.tile([P, HALF], F32, name="diff_%d_%d" % (t, h), tag=tag, align_bytes=64)
+                nc.vector.tensor_tensor(
+                    out=diff[t, h][:],
+                    in0=b_rows[t][:].indirect(entries(l_n3, h * HALF, (h + 1) * HALF)),
+                    in1=b4[t, h][:],
+                    op=ALU.subtract,
+                )
+        gate = []
+        for jb in range(4):
+            turned = ps.tile([P, PACK, P], F32, name="turned", tag="turn", bufs=2)
+            for t in range(PACK):
+                c0 = (jb % 2) * P
+                nc.tensor.transpose(turned[:, t, :], diff[t, jb // 2][:, c0 : c0 + P], ident[:])
+            g = sb.tile([P, PACK * P], F32, name="gate%d" % jb)
+            nc.scalar.activation(out=g[:], in_=turned[:].rearrange("j t p -> j (t p)"), func=ACT.Tanh)
+            gate.append(g)
+
+        rounded4 = round_weight(raw4, "rounded4")
+        q4 = quantize(rounded4[:], S, "q4")
+
+        mix = []
+        for jb in range(4):
+            bank = ps.tile([P, PACK, P], F32, name="mix%d" % jb)
+            for t in range(PACK):
+                for k, rows in enumerate((y_rows, nd_rows)):
+                    nc.tensor.matmul(
+                        bank[:, t, :], rows[t][:, jb * P : (jb + 1) * P], ident[:],
+                        start=(t == 0 and k == 0), stop=False, is_transpose=True,
+                    )
+            mix.append(bank)
+
+        h_rows = [sb.tile([P, S], F32, name="h%d" % t) for t in range(PACK)]
+        for lo, hi in MIX_PIECES:
+            w = hi - lo
+            for t in range(PACK):
+                gap = sb.tile([P, 2, w], F32, name="gap_%d_%d" % (t, lo))
+                nc.vector.tensor_tensor(
+                    out=gap[:, 0, :], in0=nd_rows[t][:].indirect(entries(l_n2, lo, hi)),
+                    in1=y_rows[t][:, lo:hi], op=ALU.add,
+                )
+                nc.vector.tensor_tensor(
+                    out=gap[:, 1, :], in0=y_rows[t][:].indirect(entries(l_n1, lo, hi)),
+                    in1=nd_rows[t][:, lo:hi], op=ALU.add,
+                )
+                rise = sb.tile([P, 2, w], F32, name="rise_%d_%d" % (t, lo))
+                nc.scalar.activation(out=rise[:], in_=gap[:], func=ACT.Relu, scale=-1.0)
+                for jb in range(lo // P, hi // P):
+                    c0 = jb * P - lo
+                    for k in range(2):
+                        nc.tensor.matmul(
+                            mix[jb][:, t, :], rise[:, k, c0 : c0 + P], ident[:],
+                            start=False, stop=(t == PACK - 1 and k == 1), is_transpose=True,
+                        )
+            z_rounded = sb.tile([P, w * PACK], BF16, name="z_rounded%d" % lo, align_bytes=64)
+            for jb in range(lo // P, hi // P):
+                z_turned = sb.tile([P, PACK * P], BF16, name="z_turned%d" % jb)
+                nc.vector.tensor_tensor(
+                    out=z_turned[:].rearrange("j (u p e) -> j u p e", u=2, e=2),
+                    in0=mix[jb][:].rearrange("j (u e) p -> j u p e", e=2),
+                    in1=gate[jb][:].rearrange("j (u e p) -> j u p e", u=2, e=2),
+                    op=ALU.mult,
+                )
+                back = ps.tile([P, 2, P], F32, name="back", tag="turn", bufs=2)
+                for u in range(2):
+                    nc.tensor.transpose(back[:, u, :], z_turned[:].bitcast(F32)[:, u * P : (u + 1) * P], ident[:])
+                c0 = (jb * P - lo) * 2
+                nc.scalar.copy(
+                    out=z_rounded[:].bitcast(F32)[:, c0 : c0 + 2 * P].rearrange("p (j u) -> p j u", u=2),
+                    in_=back[:].rearrange("p u j -> p j u"),
+                )
+            qz = quantize(z_rounded[:], w, "qz%d" % lo)
+            per_bank = S // w
+            for t0 in range(0, PACK, per_bank):
+                acc = ps.tile([P, per_bank, w], F32, name="acc", tag="acc", bufs=2)
+                for t in range(t0, t0 + per_bank):
+                    product(acc[:, t - t0, :], q4, t, qz)
+                for t in range(t0, t0 + per_bank):
+                    nc.scalar.copy(out=h_rows[t][:, lo:hi], in_=acc[:, t - t0, :])
+
+        out_rows = out.rearrange("(p t) j -> p t j", t=PACK)
+        looked = {}
+
+        def finish(t, lo, hi):
+            res = sb.tile([P, hi - lo], F32, name="res_%d_%d" % (t, lo))
+            nc.vector.tensor_tensor(out=res[:], in0=looked[t][:, lo:hi], in1=h_rows[t][:, lo:hi], op=ALU.max)
+            nc.sync.dma_start(out=out_rows[:, t, lo:hi], in_=res[:])
+
+        for t in range(PACK):
+            looked[t] = sb.tile([P, S], F32, name="looked%d" % t)
+            for h in range(2):
+                lo, hi = h * HALF, (h + 1) * HALF
+                nc.vector.tensor_copy(out=looked[t][:, lo:hi], in_=h_rows[t][:].indirect(entries(l_n5, lo, hi)))
+                if h == 0 and t > 0:
+                    finish(t - 1, 0, S)
+        finish(PACK - 1, 0, HALF)
+        finish(PACK - 1, HALF, S)

@@ -20,8 +20,6 @@ S = 512
 HALF = 256
 FLOPS = 4 * 2 * 512 * 512 * 512
 
-MIX_PIECES = ((0, 256), (256, 384), (384, 512))
-
 
 def tile_picked_triomaxbjointbbig_none_p_kernel(
     tc, x_words, x_scales, w1, w2, w3, gn, w4, offs, two, three, n1, n2, n3, n4, n5, out
@@ -37,9 +35,14 @@ def tile_picked_triomaxbjointbbig_none_p_kernel(
             nc.sync.dma_start(out=tile[:], in_=src)
             return tile
 
-        def load_weight(src, name):
-            raw = sb.tile([P, PACK, S], F32, name=name)
-            nc.sync.dma_start(out=raw[:], in_=src.rearrange("(p j) c -> p j c", j=PACK))
+        def load_weight(src, name, parts):
+            rows = src.rearrange("(p j) c -> p j c", j=PACK)
+            width = S // parts
+            raw = []
+            for part in range(parts):
+                tile = sb.tile([P, PACK, width], F32, name="%s_%d" % (name, part))
+                nc.sync.dma_start(out=tile[:], in_=rows[:, :, part * width : (part + 1) * width])
+                raw.append(tile)
             return raw
 
         def entries(tile, lo, hi):
@@ -54,20 +57,20 @@ def tile_picked_triomaxbjointbbig_none_p_kernel(
             )
         l_offs = load_list(offs, "l_offs")
         l_two = load_list(two, "l_two")
-        raw3 = load_weight(w3, "raw3")
         x_codes = sb.tile([P, T_COLS], U32, name="x_codes")
         nc.sync.dma_start(
             out=x_codes[:].bitcast(I32), in_=x_words[0].rearrange("p n t -> p (n t)").bitcast(I32)
         )
+        raw3 = load_weight(w3, "raw3", 2)
         gain = sb.tile([P, PACK], F32, name="gain")
         nc.sync.dma_start(out=gain[:], in_=gn.rearrange("(p t) o -> p (t o)", t=PACK))
         l_n4 = load_list(n4, "l_n4")
         l_n3 = load_list(n3, "l_n3")
-        raw1 = load_weight(w1, "raw1")
-        raw2 = load_weight(w2, "raw2")
+        raw1 = load_weight(w1, "raw1", 1)
+        raw2 = load_weight(w2, "raw2", 1)
         l_n2 = load_list(n2, "l_n2")
         l_n1 = load_list(n1, "l_n1")
-        raw4 = load_weight(w4, "raw4")
+        raw4 = load_weight(w4, "raw4", 1)
         l_n5 = load_list(n5, "l_n5")
 
         ident = sb.tile([P, P], F32, name="ident")
@@ -75,12 +78,18 @@ def tile_picked_triomaxbjointbbig_none_p_kernel(
         warm = sb.tile([P, 1], F32, name="warm")
         nc.scalar.activation(out=warm[:], in_=ident[:, 0:1], func=ACT.Tanh)
 
-        def round_weight(raw, tag):
+        def window(name):
+            tile = sb.tile([P, 2 * S], F32, name=name, align_bytes=64)
+            nc.vector.memset(tile[:, S:], 0.0)
+            return tile
+
+        def round_weight(raw, tag, pieces):
             rounded = sb.tile([P, PACK * S], BF16, name=tag, tag=tag, align_bytes=64)
-            nc.scalar.copy(
-                out=rounded[:].rearrange("p (t m j) -> p m j t", t=PACK, j=PACK),
-                in_=raw[:].rearrange("p j (m t) -> p m j t", t=PACK),
-            )
+            dealt = rounded[:].rearrange("p (t m j) -> p m j t", t=PACK, j=PACK)
+            step, per_part = P // pieces, P // len(raw)
+            for m0 in range(0, P, step):
+                part = raw[m0 // per_part][:].rearrange("p j (m t) -> p m j t", t=PACK)
+                nc.scalar.copy(out=dealt[:, m0 : m0 + step], in_=part[:, m0 % per_part : m0 % per_part + step])
             return rounded
 
         def quantize(rounded, width, name):
@@ -106,21 +115,21 @@ def tile_picked_triomaxbjointbbig_none_p_kernel(
                 stop=True,
             )
 
-        def project(weight, tokens, t, factor, name):
-            acc = ps.tile([P, S], F32, name="acc", tag="acc", bufs=2)
+        def project(weight, tokens, t, factor, row, bank):
+            acc = ps.tile([P, S], F32, name="acc", tag=bank)
             product(acc[:], weight, t, tokens)
-            row = sb.tile([P, S], F32, name=name)
-            nc.scalar.activation(out=row[:], in_=acc[:], func=ACT.Copy, scale=factor[:, t : t + 1])
-            return row
+            nc.scalar.activation(out=row[:, :S], in_=acc[:], func=ACT.Copy, scale=factor[:, t : t + 1])
 
         bytes3 = pick(x_bytes, l_three, U8, "bytes3")
         bytes1 = pick(x_bytes, l_offs, U8, "bytes1")
         bytes2 = pick(x_bytes, l_two, U8, "bytes2")
-        rounded3 = round_weight(raw3, "rounded3")
         codes3 = pick(x_codes, l_three, U32, "codes3")
+        codes1 = pick(x_codes, l_offs, U32, "codes1")
+        rounded3 = round_weight(raw3, "rounded3", 2)
         q3 = quantize(rounded3[:], S, "q3")
-        codes1 = pick(x_codes, l_offs, U32, "codes1", "rounded3")
-        codes2 = pick(x_codes, l_two, U32, "codes2")
+        codes2 = pick(x_codes, l_two, U32, "codes2", "rounded3")
+
+        b_rows = [window("b%d" % t) for t in range(PACK)]
 
         g_sign = sb.tile([P, PACK], F32, name="g_sign")
         g_abs = sb.tile([P, PACK], F32, name="g_abs")
@@ -129,121 +138,139 @@ def tile_picked_triomaxbjointbbig_none_p_kernel(
         nc.scalar.activation(out=g_abs[:], in_=gain[:], func=ACT.Abs)
         nc.scalar.activation(out=g_neg[:], in_=g_abs[:], func=ACT.Copy, scale=-1.0)
 
-        b_rows = [project(q3, (codes3, bytes3), t, g_sign, "b%d" % t) for t in range(PACK)]
-        rounded1 = round_weight(raw1, "rounded1")
-        rounded2 = round_weight(raw2, "rounded2")
+        for t in range(PACK):
+            project(q3, (codes3, bytes3), t, g_sign, b_rows[t], "work%d" % t)
+        rounded1 = round_weight(raw1, "rounded1", 4)
+        rounded2 = round_weight(raw2, "rounded2", 2)
         q1 = quantize(rounded1[:], S, "q1")
         q2 = quantize(rounded2[:], S, "q2")
-        y_rows, nd_rows = [], []
+        y_rows = [
+            sb.tile([P, 2 * S], F32, name="y", tag="rounded1" if t == 3 else "y%d" % t, align_bytes=64)
+            for t in range(PACK)
+        ]
+        nd_rows = [
+            sb.tile([P, 2 * S], F32, name="nd", tag="rounded2" if t == 1 else "nd%d" % t, align_bytes=64)
+            for t in range(PACK)
+        ]
         for t in range(PACK):
-            y_rows.append(project(q1, (codes1, bytes1), t, g_abs, "y%d" % t))
-            nd_rows.append(project(q2, (codes2, bytes2), t, g_neg, "nd%d" % t))
+            project(q1, (codes1, bytes1), t, g_abs, y_rows[t], "work%d" % (2 * t % 4))
+            project(q2, (codes2, bytes2), t, g_neg, nd_rows[t], "work%d" % ((2 * t + 1) % 4))
+        rounded4 = round_weight(raw4, "rounded4", 4)
 
-        b4 = {}
+        b4 = [y_rows[t][:, S:] for t in range(PACK)]
+        diff = [nd_rows[t][:, S:] for t in range(PACK)]
         for t in range(PACK):
-            for h in range(2):
-                tag = "rounded1" if (t, h) == (3, 0) else "b4_%d_%d" % (t, h)
-                b4[t, h] = sb.tile([P, HALF], F32, name="b4_%d_%d" % (t, h), tag=tag, align_bytes=64)
-                nc.vector.tensor_copy(
-                    out=b4[t, h][:], in_=b_rows[t][:].indirect(entries(l_n4, h * HALF, (h + 1) * HALF))
-                )
-        diff = {}
-        for h in range(2):
-            for t in range(PACK):
-                tag = "rounded2" if (t, h) == (3, 0) else "diff_%d_%d" % (t, h)
-                diff[t, h] = sb.tile([P, HALF], F32, name="diff_%d_%d" % (t, h), tag=tag, align_bytes=64)
-                nc.vector.tensor_tensor(
-                    out=diff[t, h][:],
-                    in0=b_rows[t][:].indirect(entries(l_n3, h * HALF, (h + 1) * HALF)),
-                    in1=b4[t, h][:],
-                    op=ALU.subtract,
-                )
-        gate = []
-        for jb in range(4):
-            turned = ps.tile([P, PACK, P], F32, name="turned", tag="turn", bufs=2)
-            for t in range(PACK):
-                c0 = (jb % 2) * P
-                nc.tensor.transpose(turned[:, t, :], diff[t, jb // 2][:, c0 : c0 + P], ident[:])
-            g = sb.tile([P, PACK * P], F32, name="gate%d" % jb)
-            nc.scalar.activation(out=g[:], in_=turned[:].rearrange("j t p -> j (t p)"), func=ACT.Tanh)
-            gate.append(g)
+            nc.vector.tensor_copy(out=b4[t], in_=b_rows[t][:].indirect(l_n4[:]))
+        for t in range(PACK):
+            nc.vector.tensor_tensor(out=diff[t], in0=b_rows[t][:].indirect(l_n3[:]), in1=b4[t], op=ALU.subtract)
 
-        rounded4 = round_weight(raw4, "rounded4")
-        q4 = quantize(rounded4[:], S, "q4")
+        mix = {}
+        for u in range(2):
+            for jp in range(2):
+                bank = ps.tile([P, 2, 2, P], F32, name="mix", tag="mix%d%d" % (u, jp))
+                for e in range(2):
+                    for k, rows in enumerate((y_rows, nd_rows)):
+                        for b in range(2):
+                            jb = 2 * jp + b
+                            nc.tensor.matmul(
+                                bank[:, b, e, :], rows[2 * u + e][:, jb * P : (jb + 1) * P], ident[:],
+                                start=(e == 0 and k == 0 and b == 0), stop=False, is_transpose=True,
+                            )
+                mix[u, jp] = bank
 
-        mix = []
-        for jb in range(4):
-            bank = ps.tile([P, PACK, P], F32, name="mix%d" % jb)
-            for t in range(PACK):
-                for k, rows in enumerate((y_rows, nd_rows)):
-                    nc.tensor.matmul(
-                        bank[:, t, :], rows[t][:, jb * P : (jb + 1) * P], ident[:],
-                        start=(t == 0 and k == 0), stop=False, is_transpose=True,
-                    )
-            mix.append(bank)
+        gate = [sb.tile([P, 2, 2, P, 2], F32, name="gate%d" % jp, align_bytes=64) for jp in range(2)]
 
-        h_rows = [sb.tile([P, S], F32, name="h%d" % t) for t in range(PACK)]
-        for lo, hi in MIX_PIECES:
-            w = hi - lo
+        def make_gate(jb):
+            turned = ps.tile([P, PACK, P], F32, name="turned", tag="work%d" % jb)
             for t in range(PACK):
-                gap = sb.tile([P, 2, w], F32, name="gap_%d_%d" % (t, lo))
-                nc.vector.tensor_tensor(
-                    out=gap[:, 0, :], in0=nd_rows[t][:].indirect(entries(l_n2, lo, hi)),
-                    in1=y_rows[t][:, lo:hi], op=ALU.add,
-                )
-                nc.vector.tensor_tensor(
-                    out=gap[:, 1, :], in0=y_rows[t][:].indirect(entries(l_n1, lo, hi)),
-                    in1=nd_rows[t][:, lo:hi], op=ALU.add,
-                )
-                rise = sb.tile([P, 2, w], F32, name="rise_%d_%d" % (t, lo))
-                nc.scalar.activation(out=rise[:], in_=gap[:], func=ACT.Relu, scale=-1.0)
+                nc.tensor.transpose(turned[:, t, :], diff[t][:, jb * P : (jb + 1) * P], ident[:])
+            nc.scalar.activation(
+                out=gate[jb // 2][:, :, jb % 2, :, :],
+                in_=turned[:].rearrange("j (u e) p -> j u p e", e=2),
+                func=ACT.Tanh,
+            )
+
+        for t in range(PACK):
+            gap = sb.tile([P, 2, S], F32, name="gap%d" % t)
+            nc.vector.tensor_tensor(
+                out=gap[:, 0, :], in0=nd_rows[t][:].indirect(l_n2[:]), in1=y_rows[t][:, :S], op=ALU.add
+            )
+            nc.vector.tensor_tensor(
+                out=gap[:, 1, :], in0=y_rows[t][:].indirect(l_n1[:]), in1=nd_rows[t][:, :S], op=ALU.add
+            )
+            make_gate(t)
+            rise = sb.tile([P, 2, S], F32, name="rise%d" % t)
+            for lo, hi in ((0, HALF), (HALF, S)) if t == PACK - 1 else ((0, S),):
+                nc.scalar.activation(out=rise[:, :, lo:hi], in_=gap[:, :, lo:hi], func=ACT.Relu, scale=-1.0)
                 for jb in range(lo // P, hi // P):
-                    c0 = jb * P - lo
                     for k in range(2):
                         nc.tensor.matmul(
-                            mix[jb][:, t, :], rise[:, k, c0 : c0 + P], ident[:],
-                            start=False, stop=(t == PACK - 1 and k == 1), is_transpose=True,
+                            mix[t // 2, jb // 2][:, jb % 2, t % 2, :], rise[:, k, jb * P : (jb + 1) * P], ident[:],
+                            start=False, stop=(t % 2 == 1 and jb % 2 == 1 and k == 1), is_transpose=True,
                         )
-            z_rounded = sb.tile([P, w * PACK], BF16, name="z_rounded%d" % lo, align_bytes=64)
-            for jb in range(lo // P, hi // P):
-                z_turned = sb.tile([P, PACK * P], BF16, name="z_turned%d" % jb)
-                nc.vector.tensor_tensor(
-                    out=z_turned[:].rearrange("j (u p e) -> j u p e", u=2, e=2),
-                    in0=mix[jb][:].rearrange("j (u e) p -> j u p e", e=2),
-                    in1=gate[jb][:].rearrange("j (u e p) -> j u p e", u=2, e=2),
-                    op=ALU.mult,
-                )
-                back = ps.tile([P, 2, P], F32, name="back", tag="turn", bufs=2)
-                for u in range(2):
-                    nc.tensor.transpose(back[:, u, :], z_turned[:].bitcast(F32)[:, u * P : (u + 1) * P], ident[:])
-                c0 = (jb * P - lo) * 2
-                nc.scalar.copy(
-                    out=z_rounded[:].bitcast(F32)[:, c0 : c0 + 2 * P].rearrange("p (j u) -> p j u", u=2),
-                    in_=back[:].rearrange("p u j -> p j u"),
-                )
-            qz = quantize(z_rounded[:], w, "qz%d" % lo)
-            per_bank = S // w
-            for t0 in range(0, PACK, per_bank):
-                acc = ps.tile([P, per_bank, w], F32, name="acc", tag="acc", bufs=2)
-                for t in range(t0, t0 + per_bank):
-                    product(acc[:, t - t0, :], q4, t, qz)
-                for t in range(t0, t0 + per_bank):
-                    nc.scalar.copy(out=h_rows[t][:, lo:hi], in_=acc[:, t - t0, :])
+
+        z_turned = {}
+
+        def mix_times_gate(u, jp, b0, b1):
+            tile = sb.tile([P, b1 - b0, P, 2], BF16, name="z_turned_%d_%d_%d" % (u, jp, b0))
+            nc.vector.tensor_tensor(
+                out=tile[:],
+                in0=mix[u, jp][:, b0:b1].rearrange("j b e p -> j b p e"),
+                in1=gate[jp][:, u, b0:b1],
+                op=ALU.mult,
+            )
+            for b in range(b0, b1):
+                z_turned[u, 2 * jp + b] = tile[:, b - b0].rearrange("j p e -> j (p e)").bitcast(F32)
+
+        def turn_back(jb0, jb1, bank):
+            n = jb1 - jb0
+            back = ps.tile([P, n, 2, P], F32, name="back", tag=bank)
+            for u in range(2):
+                for jb in range(jb0, jb1):
+                    nc.tensor.transpose(back[:, jb - jb0, u, :], z_turned[u, jb], ident[:])
+            rounded = sb.tile([P, n * P * PACK], BF16, name="z_rounded%d" % jb0, align_bytes=64)
+            nc.scalar.copy(
+                out=rounded[:].bitcast(F32).rearrange("p (b j u) -> p b j u", b=n, u=2),
+                in_=back[:].rearrange("p b u j -> p b j u"),
+            )
+            return quantize(rounded[:], n * P, "qz%d" % jb0)
+
+        for u in range(2):
+            for jp in range(2):
+                mix_times_gate(u, jp, 0, 2)
+        q4_codes = sb.tile([P, S], U32, name="q4_codes", tag="gate1", align_bytes=64)
+        q4_scales = sb.tile([P, S], U8, name="q4_scales", align_bytes=64)
+        nc.vector.quantize_mx(out=q4_codes[:].bitcast(FP8X4), scales=q4_scales[:], in_=rounded4[:])
+        q4 = (q4_codes, q4_scales)
+
+        qz = [turn_back(0, 2, "work0"), turn_back(2, 4, "work1")]
+
+        h_rows = b_rows
+        for jp, bank in enumerate(("work2", "mix00")):
+            acc = ps.tile([P, HALF], F32, name="acc", tag=bank)
+            product(acc[:], q4, 0, qz[jp])
+            nc.scalar.copy(out=h_rows[0][:, jp * HALF : (jp + 1) * HALF], in_=acc[:])
+        for t, bank in ((1, "work3"), (2, "mix01"), (3, "mix10")):
+            acc = ps.tile([P, 2, HALF], F32, name="acc", tag=bank)
+            for jp in range(2):
+                product(acc[:, jp, :], q4, t, qz[jp])
+            nc.scalar.copy(out=h_rows[t][:, :S], in_=acc[:].rearrange("p a b -> p (a b)"))
 
         out_rows = out.rearrange("(p t) j -> p t j", t=PACK)
         looked = {}
 
+        def look(t, lo, hi):
+            looked[t, lo] = sb.tile([P, hi - lo], F32, name="looked_%d_%d" % (t, lo))
+            nc.vector.tensor_copy(out=looked[t, lo][:], in_=h_rows[t][:].indirect(entries(l_n5, lo, hi)))
+
         def finish(t, lo, hi):
             res = sb.tile([P, hi - lo], F32, name="res_%d_%d" % (t, lo))
-            nc.vector.tensor_tensor(out=res[:], in0=looked[t][:, lo:hi], in1=h_rows[t][:, lo:hi], op=ALU.max)
+            nc.vector.tensor_tensor(out=res[:], in0=looked[t, lo][:], in1=h_rows[t][:, lo:hi], op=ALU.max)
             nc.sync.dma_start(out=out_rows[:, t, lo:hi], in_=res[:])
 
-        for t in range(PACK):
-            looked[t] = sb.tile([P, S], F32, name="looked%d" % t)
-            for h in range(2):
-                lo, hi = h * HALF, (h + 1) * HALF
-                nc.vector.tensor_copy(out=looked[t][:, lo:hi], in_=h_rows[t][:].indirect(entries(l_n5, lo, hi)))
-                if h == 0 and t > 0:
-                    finish(t - 1, 0, S)
-        finish(PACK - 1, 0, HALF)
-        finish(PACK - 1, HALF, S)
+        steps = [(0, 0, S), (1, 0, S), (2, 0, S), (3, 0, HALF), (3, HALF, S)]
+        for i, step in enumerate(steps):
+            look(*step)
+            if i > 0:
+                finish(*steps[i - 1])
+        finish(*steps[-1])

@@ -40,7 +40,7 @@ def tile_picked_triomaxbjointbbig_none_p_kernel(
             width = S // parts
             raw = []
             for part in range(parts):
-                tile = sb.tile([P, PACK, width], F32, name="%s_%d" % (name, part))
+                tile = sb.tile([P, PACK, width], F32, name="%s_%d" % (name, part), align_bytes=64)
                 nc.sync.dma_start(out=tile[:], in_=rows[:, :, part * width : (part + 1) * width])
                 raw.append(tile)
             return raw
@@ -130,6 +130,7 @@ def tile_picked_triomaxbjointbbig_none_p_kernel(
         codes2 = pick(x_codes, l_two, U32, "codes2", "rounded3")
 
         b_rows = [window("b%d" % t) for t in range(PACK)]
+        y1_row = window("y1")
 
         g_sign = sb.tile([P, PACK], F32, name="g_sign")
         g_abs = sb.tile([P, PACK], F32, name="g_abs")
@@ -145,19 +146,19 @@ def tile_picked_triomaxbjointbbig_none_p_kernel(
         q1 = quantize(rounded1[:], S, "q1")
         q2 = quantize(rounded2[:], S, "q2")
         y_rows = [
-            sb.tile([P, 2 * S], F32, name="y", tag="rounded1" if t == 3 else "y%d" % t, align_bytes=64)
-            for t in range(PACK)
+            y1_row if t == 1 else sb.tile([P, 2 * S], F32, name="y", tag=tag, align_bytes=64)
+            for t, tag in enumerate(("y0", "y1", "y2", "rounded1"))
         ]
         nd_rows = [
-            sb.tile([P, 2 * S], F32, name="nd", tag="rounded2" if t == 1 else "nd%d" % t, align_bytes=64)
-            for t in range(PACK)
+            sb.tile([P, 2 * S], F32, name="nd", tag=tag, align_bytes=64)
+            for tag in ("raw1_0", "rounded2", "raw2_0", "nd3")
         ]
         for t in range(PACK):
             project(q1, (codes1, bytes1), t, g_abs, y_rows[t], "work%d" % (2 * t % 4))
             project(q2, (codes2, bytes2), t, g_neg, nd_rows[t], "work%d" % ((2 * t + 1) % 4))
         rounded4 = round_weight(raw4, "rounded4", 4)
 
-        b4 = [y_rows[t][:, S:] for t in range(PACK)]
+        b4 = [(nd_rows[3] if t == 1 else y_rows[t])[:, S:] for t in range(PACK)]
         diff = [nd_rows[t][:, S:] for t in range(PACK)]
         for t in range(PACK):
             nc.vector.tensor_copy(out=b4[t], in_=b_rows[t][:].indirect(l_n4[:]))
@@ -181,7 +182,7 @@ def tile_picked_triomaxbjointbbig_none_p_kernel(
         gate = [sb.tile([P, 2, 2, P, 2], F32, name="gate%d" % jp, align_bytes=64) for jp in range(2)]
 
         def make_gate(jb):
-            turned = ps.tile([P, PACK, P], F32, name="turned", tag="work%d" % jb)
+            turned = ps.tile([P, PACK, P], F32, name="turned", tag=("work3", "work1")[jb % 2])
             for t in range(PACK):
                 nc.tensor.transpose(turned[:, t, :], diff[t][:, jb * P : (jb + 1) * P], ident[:])
             nc.scalar.activation(
@@ -192,15 +193,17 @@ def tile_picked_triomaxbjointbbig_none_p_kernel(
 
         for t in range(PACK):
             gap = sb.tile([P, 2, S], F32, name="gap%d" % t)
-            nc.vector.tensor_tensor(
-                out=gap[:, 0, :], in0=nd_rows[t][:].indirect(l_n2[:]), in1=y_rows[t][:, :S], op=ALU.add
-            )
-            nc.vector.tensor_tensor(
-                out=gap[:, 1, :], in0=y_rows[t][:].indirect(l_n1[:]), in1=nd_rows[t][:, :S], op=ALU.add
-            )
-            make_gate(t)
             rise = sb.tile([P, 2, S], F32, name="rise%d" % t)
+            make_gate(t)
             for lo, hi in ((0, HALF), (HALF, S)) if t == PACK - 1 else ((0, S),):
+                nc.vector.tensor_tensor(
+                    out=gap[:, 0, lo:hi], in0=nd_rows[t][:].indirect(entries(l_n2, lo, hi)),
+                    in1=y_rows[t][:, lo:hi], op=ALU.add,
+                )
+                nc.vector.tensor_tensor(
+                    out=gap[:, 1, lo:hi], in0=y_rows[t][:].indirect(entries(l_n1, lo, hi)),
+                    in1=nd_rows[t][:, lo:hi], op=ALU.add,
+                )
                 nc.scalar.activation(out=rise[:, :, lo:hi], in_=gap[:, :, lo:hi], func=ACT.Relu, scale=-1.0)
                 for jb in range(lo // P, hi // P):
                     for k in range(2):
@@ -210,6 +213,8 @@ def tile_picked_triomaxbjointbbig_none_p_kernel(
                         )
 
         z_turned = {}
+        z_codes = sb.tile([P, S], U32, name="z_codes", align_bytes=64)
+        z_scales = sb.tile([P, S], U8, name="z_scales", align_bytes=64)
 
         def mix_times_gate(u, jp, b0, b1):
             tile = sb.tile([P, b1 - b0, P, 2], BF16, name="z_turned_%d_%d_%d" % (u, jp, b0))
@@ -233,28 +238,39 @@ def tile_picked_triomaxbjointbbig_none_p_kernel(
                 out=rounded[:].bitcast(F32).rearrange("p (b j u) -> p b j u", b=n, u=2),
                 in_=back[:].rearrange("p b u j -> p b j u"),
             )
-            return quantize(rounded[:], n * P, "qz%d" % jb0)
+            cols = slice(jb0 * P, jb1 * P)
+            nc.vector.quantize_mx(out=z_codes[:, cols].bitcast(FP8X4), scales=z_scales[:, cols], in_=rounded[:])
 
-        for u in range(2):
-            for jp in range(2):
-                mix_times_gate(u, jp, 0, 2)
-        q4_codes = sb.tile([P, S], U32, name="q4_codes", tag="gate1", align_bytes=64)
-        q4_scales = sb.tile([P, S], U8, name="q4_scales", align_bytes=64)
-        nc.vector.quantize_mx(out=q4_codes[:].bitcast(FP8X4), scales=q4_scales[:], in_=rounded4[:])
-        q4 = (q4_codes, q4_scales)
+        mix_times_gate(0, 0, 0, 2)
+        mix_times_gate(0, 1, 0, 2)
+        mix_times_gate(1, 0, 0, 2)
+        mix_times_gate(1, 1, 0, 1)
+        mix_times_gate(1, 1, 1, 2)
+        def quantize_w4(pair, tag):
+            codes = sb.tile([P, HALF], U32, name="q4_codes", tag=tag, align_bytes=64)
+            scales = sb.tile([P, HALF], U8, name="q4_scales%d" % pair, align_bytes=64)
+            in_ = rounded4[:, pair * PACK * HALF : (pair + 1) * PACK * HALF]
+            nc.vector.quantize_mx(out=codes[:].bitcast(FP8X4), scales=scales[:], in_=in_)
+            return codes, scales
 
-        qz = [turn_back(0, 2, "work0"), turn_back(2, 4, "work1")]
+        q4 = [quantize_w4(0, "gate1")]
+        turn_back(0, 2, "work0")
+        turn_back(2, 3, "work1")
+        turn_back(3, 4, "mix01")
+        q4.append(quantize_w4(1, "z_rounded3"))
 
         h_rows = b_rows
-        for jp, bank in enumerate(("work2", "mix00")):
-            acc = ps.tile([P, HALF], F32, name="acc", tag=bank)
-            product(acc[:], q4, 0, qz[jp])
-            nc.scalar.copy(out=h_rows[0][:, jp * HALF : (jp + 1) * HALF], in_=acc[:])
-        for t, bank in ((1, "work3"), (2, "mix01"), (3, "mix10")):
-            acc = ps.tile([P, 2, HALF], F32, name="acc", tag=bank)
-            for jp in range(2):
-                product(acc[:, jp, :], q4, t, qz[jp])
-            nc.scalar.copy(out=h_rows[t][:, :S], in_=acc[:].rearrange("p a b -> p (a b)"))
+        for lo, hi, bank in ((0, 2 * P, "work2"), (2 * P, 3 * P, "mix00"), (3 * P, S, "mix10")):
+            acc = ps.tile([P, hi - lo], F32, name="acc", tag=bank)
+            product(acc[:], q4[0], 0, (z_codes[:, lo:hi], z_scales[:, lo:hi]))
+            if hi == S:
+                nc.vector.tensor_copy(out=h_rows[0][:, lo:hi], in_=acc[:])
+            else:
+                nc.scalar.copy(out=h_rows[0][:, lo:hi], in_=acc[:])
+        for t, bank in ((1, "work3"), (2, "work0"), (3, "mix11")):
+            acc = ps.tile([P, S], F32, name="acc", tag=bank)
+            product(acc[:], q4[t // 2], t % 2, (z_codes, z_scales))
+            nc.scalar.copy(out=h_rows[t][:, :S], in_=acc[:])
 
         out_rows = out.rearrange("(p t) j -> p t j", t=PACK)
         looked = {}

@@ -57,11 +57,11 @@ def tile_picked_triomaxbjointbbig_none_p_kernel(
             )
         l_offs = load_list(offs, "l_offs")
         l_two = load_list(two, "l_two")
+        raw3 = load_weight(w3, "raw3", 2)
         x_codes = sb.tile([P, T_COLS], U32, name="x_codes")
         nc.sync.dma_start(
             out=x_codes[:].bitcast(I32), in_=x_words[0].rearrange("p n t -> p (n t)").bitcast(I32)
         )
-        raw3 = load_weight(w3, "raw3", 2)
         gain = sb.tile([P, PACK], F32, name="gain")
         nc.sync.dma_start(out=gain[:], in_=gn.rearrange("(p t) o -> p (t o)", t=PACK))
         l_n4 = load_list(n4, "l_n4")
@@ -123,11 +123,11 @@ def tile_picked_triomaxbjointbbig_none_p_kernel(
         bytes3 = pick(x_bytes, l_three, U8, "bytes3")
         bytes1 = pick(x_bytes, l_offs, U8, "bytes1")
         bytes2 = pick(x_bytes, l_two, U8, "bytes2")
-        codes3 = pick(x_codes, l_three, U32, "codes3")
-        codes1 = pick(x_codes, l_offs, U32, "codes1")
         rounded3 = round_weight(raw3, "rounded3", 2)
         q3 = quantize(rounded3[:], S, "q3")
-        codes2 = pick(x_codes, l_two, U32, "codes2", "rounded3")
+        codes3 = pick(x_codes, l_three, U32, "codes3")
+        codes1 = pick(x_codes, l_offs, U32, "codes1", "rounded3")
+        codes2 = pick(x_codes, l_two, U32, "codes2")
 
         b_rows = [window("b%d" % t) for t in range(PACK)]
         y1_row = window("y1")

@@ -15,9 +15,11 @@ ALU = mybir.AluOpType
 
 P = 128
 PACK = 4
-T_COLS = 2048
+TOKENS = 2048
 S = 512
-HALF = 256
+HALF = S // 2
+GROUP = 16
+QUADRANT = 32
 FLOPS = 4 * 2 * 512 * 512 * 512
 
 
@@ -31,60 +33,57 @@ def tile_picked_triomaxbjointbbig_none_p_kernel(
         ps = ctx.enter_context(tc.psum_pool(name="ps", bufs=1))
 
         def load_list(src, name):
-            tile = lists.tile([P, S // 16], U16, name=name)
+            tile = lists.tile([P, S // GROUP], U16, name=name)
             nc.sync.dma_start(out=tile[:], in_=src)
             return tile
 
-        def load_weight(src, name, parts):
-            rows = src.rearrange("(p j) c -> p j c", j=PACK)
-            width = S // parts
-            raw = []
-            for part in range(parts):
-                tile = sb.tile([P, PACK, width], F32, name="%s_%d" % (name, part), align_bytes=64)
-                nc.sync.dma_start(out=tile[:], in_=rows[:, :, part * width : (part + 1) * width])
-                raw.append(tile)
-            return raw
+        def load_columns(src, name, lo, hi):
+            tile = sb.tile([P, PACK, hi - lo], F32, name=name, align_bytes=64)
+            nc.sync.dma_start(out=tile[:], in_=src.rearrange("(p j) c -> p j c", j=PACK)[:, :, lo:hi])
+            return tile
 
         def entries(tile, lo, hi):
-            return tile[:, lo // 16 : hi // 16]
+            return tile[:, lo // GROUP : hi // GROUP]
 
         l_three = load_list(three, "l_three")
-        x_bytes = sb.tile([P, T_COLS], U8, name="x_bytes")
-        for q in range(4):
+        x_bytes = sb.tile([P, TOKENS], U8, name="x_bytes")
+        for q in range(P // QUADRANT):
             nc.sync.dma_start(
-                out=x_bytes[32 * q : 32 * q + 32, :].bitcast(I32),
-                in_=x_scales[0, 4 * q : 4 * q + 4, :].bitcast(I32).partition_broadcast(8),
+                out=x_bytes[QUADRANT * q : QUADRANT * (q + 1), :].bitcast(I32),
+                in_=x_scales[0, 4 * q : 4 * q + 4, :].bitcast(I32).partition_broadcast(QUADRANT // 4),
             )
+        gain = sb.tile([P, PACK], F32, name="gain")
+        nc.sync.dma_start(out=gain[:], in_=gn.rearrange("(p t) o -> p (t o)", t=PACK))
+        raw3 = [load_columns(w3, "raw3_left", 0, HALF)]
         l_offs = load_list(offs, "l_offs")
         l_two = load_list(two, "l_two")
-        raw3 = load_weight(w3, "raw3", 2)
-        x_codes = sb.tile([P, T_COLS], U32, name="x_codes")
+        raw3.append(load_columns(w3, "raw3_right", HALF, S))
+        x_codes = sb.tile([P, TOKENS], U32, name="x_codes")
         nc.sync.dma_start(
             out=x_codes[:].bitcast(I32), in_=x_words[0].rearrange("p n t -> p (n t)").bitcast(I32)
         )
-        gain = sb.tile([P, PACK], F32, name="gain")
-        nc.sync.dma_start(out=gain[:], in_=gn.rearrange("(p t) o -> p (t o)", t=PACK))
         l_n4 = load_list(n4, "l_n4")
         l_n3 = load_list(n3, "l_n3")
-        raw1 = load_weight(w1, "raw1", 1)
-        raw2 = load_weight(w2, "raw2", 1)
+        raw1 = [load_columns(w1, "raw1", 0, S)]
+        raw2 = [load_columns(w2, "raw2", 0, S)]
         l_n2 = load_list(n2, "l_n2")
         l_n1 = load_list(n1, "l_n1")
-        raw4 = load_weight(w4, "raw4", 1)
+        raw4 = [load_columns(w4, "raw4", 0, S)]
         l_n5 = load_list(n5, "l_n5")
 
         ident = sb.tile([P, P], F32, name="ident")
         make_identity(nc, ident[:])
-        warm = sb.tile([P, 1], F32, name="warm")
-        nc.scalar.activation(out=warm[:], in_=ident[:, 0:1], func=ACT.Tanh)
 
-        def window(name):
-            tile = sb.tile([P, 2 * S], F32, name=name, align_bytes=64)
+        def window(name, tag):
+            return sb.tile([P, 2 * S], F32, name=name, tag=tag, align_bytes=64)
+
+        def cleared_window(name):
+            tile = window(name, name)
             nc.vector.memset(tile[:, S:], 0.0)
             return tile
 
-        def round_weight(raw, tag, pieces):
-            rounded = sb.tile([P, PACK * S], BF16, name=tag, tag=tag, align_bytes=64)
+        def round_weight(raw, name, pieces):
+            rounded = sb.tile([P, PACK * S], BF16, name=name, align_bytes=64)
             dealt = rounded[:].rearrange("p (t m j) -> p m j t", t=PACK, j=PACK)
             step, per_part = P // pieces, P // len(raw)
             for m0 in range(0, P, step):
@@ -92,19 +91,20 @@ def tile_picked_triomaxbjointbbig_none_p_kernel(
                 nc.scalar.copy(out=dealt[:, m0 : m0 + step], in_=part[:, m0 % per_part : m0 % per_part + step])
             return rounded
 
-        def quantize(rounded, width, name):
-            codes = sb.tile([P, width], U32, name=name + "_codes", align_bytes=64)
+        def quantize_weight(rounded, name, codes_tag):
+            width = rounded.shape[1] // PACK
+            codes = sb.tile([P, width], U32, name=name + "_codes", tag=codes_tag, align_bytes=64)
             scales = sb.tile([P, width], U8, name=name + "_scales", align_bytes=64)
             nc.vector.quantize_mx(out=codes[:].bitcast(FP8X4), scales=scales[:], in_=rounded)
             return codes, scales
 
-        def pick(window, lst, dtype, name, tag=""):
-            picked = sb.tile([P, S], dtype, name=name, tag=tag or name, align_bytes=64)
-            nc.vector.tensor_copy(out=picked[:], in_=window[:].indirect(lst[:]))
+        def pick(table, token_list, dtype, tag):
+            picked = sb.tile([P, S], dtype, name="picked", tag=tag, align_bytes=64)
+            nc.vector.tensor_copy(out=picked[:], in_=table[:].indirect(token_list[:]))
             return picked
 
-        def product(acc, weight, t, moving):
-            cols = slice(t * P, (t + 1) * P)
+        def product(acc, weight, block, moving):
+            cols = slice(block * P, (block + 1) * P)
             nc.tensor.matmul_mx(
                 out=acc,
                 lhsT=weight[0][:, cols].bitcast(FP8X4),
@@ -120,18 +120,6 @@ def tile_picked_triomaxbjointbbig_none_p_kernel(
             product(acc[:], weight, t, tokens)
             nc.scalar.activation(out=row[:, :S], in_=acc[:], func=ACT.Copy, scale=factor[:, t : t + 1])
 
-        bytes3 = pick(x_bytes, l_three, U8, "bytes3")
-        bytes1 = pick(x_bytes, l_offs, U8, "bytes1")
-        bytes2 = pick(x_bytes, l_two, U8, "bytes2")
-        rounded3 = round_weight(raw3, "rounded3", 2)
-        q3 = quantize(rounded3[:], S, "q3")
-        codes3 = pick(x_codes, l_three, U32, "codes3")
-        codes1 = pick(x_codes, l_offs, U32, "codes1", "rounded3")
-        codes2 = pick(x_codes, l_two, U32, "codes2")
-
-        b_rows = [window("b%d" % t) for t in range(PACK)]
-        y1_row = window("y1")
-
         g_sign = sb.tile([P, PACK], F32, name="g_sign")
         g_abs = sb.tile([P, PACK], F32, name="g_abs")
         g_neg = sb.tile([P, PACK], F32, name="g_neg")
@@ -139,43 +127,48 @@ def tile_picked_triomaxbjointbbig_none_p_kernel(
         nc.scalar.activation(out=g_abs[:], in_=gain[:], func=ACT.Abs)
         nc.scalar.activation(out=g_neg[:], in_=g_abs[:], func=ACT.Copy, scale=-1.0)
 
+        bytes3 = pick(x_bytes, l_three, U8, "bytes3")
+        bytes1 = pick(x_bytes, l_offs, U8, "bytes1")
+        bytes2 = pick(x_bytes, l_two, U8, "bytes2")
+        rounded3 = round_weight(raw3, "rounded3", len(raw3))
+        q3 = quantize_weight(rounded3[:], "q3", "q3_codes")
+        codes3 = pick(x_codes, l_three, U32, "codes3")
+        codes1 = pick(x_codes, l_offs, U32, "rounded3")
+        codes2 = pick(x_codes, l_two, U32, "codes2")
+
+        b_rows = [cleared_window("b%d" % t) for t in range(PACK)]
+        y1_row = cleared_window("y1")
         for t in range(PACK):
             project(q3, (codes3, bytes3), t, g_sign, b_rows[t], "work%d" % t)
         rounded1 = round_weight(raw1, "rounded1", 4)
         rounded2 = round_weight(raw2, "rounded2", 2)
-        q1 = quantize(rounded1[:], S, "q1")
-        q2 = quantize(rounded2[:], S, "q2")
-        y_rows = [
-            y1_row if t == 1 else sb.tile([P, 2 * S], F32, name="y", tag=tag, align_bytes=64)
-            for t, tag in enumerate(("y0", "y1", "y2", "rounded1"))
-        ]
-        nd_rows = [
-            sb.tile([P, 2 * S], F32, name="nd", tag=tag, align_bytes=64)
-            for tag in ("raw1_0", "rounded2", "raw2_0", "nd3")
-        ]
+        q1 = quantize_weight(rounded1[:], "q1", "q1_codes")
+        q2 = quantize_weight(rounded2[:], "q2", "q2_codes")
+        y_rows = [window("y0", "y0"), y1_row, window("y2", "y2"), window("y3", "rounded1")]
+        nd_rows = [window("nd0", "raw1"), window("nd1", "rounded2"), window("nd2", "raw2"), window("nd3", "nd3")]
         for t in range(PACK):
             project(q1, (codes1, bytes1), t, g_abs, y_rows[t], "work%d" % (2 * t % 4))
             project(q2, (codes2, bytes2), t, g_neg, nd_rows[t], "work%d" % ((2 * t + 1) % 4))
         rounded4 = round_weight(raw4, "rounded4", 4)
 
-        b4 = [(nd_rows[3] if t == 1 else y_rows[t])[:, S:] for t in range(PACK)]
-        diff = [nd_rows[t][:, S:] for t in range(PACK)]
+        b_n4 = [rows[:, S:] for rows in (y_rows[0], nd_rows[3], y_rows[2], y_rows[3])]
+        diff = [rows[:, S:] for rows in nd_rows]
         for t in range(PACK):
-            nc.vector.tensor_copy(out=b4[t], in_=b_rows[t][:].indirect(l_n4[:]))
+            nc.vector.tensor_copy(out=b_n4[t], in_=b_rows[t][:].indirect(l_n4[:]))
         for t in range(PACK):
-            nc.vector.tensor_tensor(out=diff[t], in0=b_rows[t][:].indirect(l_n3[:]), in1=b4[t], op=ALU.subtract)
+            nc.vector.tensor_tensor(out=diff[t], in0=b_rows[t][:].indirect(l_n3[:]), in1=b_n4[t], op=ALU.subtract)
 
         mix = {}
         for u in range(2):
             for jp in range(2):
                 bank = ps.tile([P, 2, 2, P], F32, name="mix", tag="mix%d%d" % (u, jp))
                 for e in range(2):
-                    for k, rows in enumerate((y_rows, nd_rows)):
-                        for b in range(2):
-                            jb = 2 * jp + b
+                    for term, rows in enumerate((y_rows, nd_rows)):
+                        for s in range(2):
+                            jb = 2 * jp + s
                             nc.tensor.matmul(
-                                bank[:, b, e, :], rows[2 * u + e][:, jb * P : (jb + 1) * P], ident[:],
-                                start=(e == 0 and k == 0 and b == 0), stop=False, is_transpose=True,
+                                bank[:, s, e, :], rows[2 * u + e][:, jb * P : (jb + 1) * P], ident[:],
+                                start=(e == 0 and term == 0 and s == 0), stop=False, is_transpose=True,
                             )
                 mix[u, jp] = bank
 
@@ -194,7 +187,9 @@ def tile_picked_triomaxbjointbbig_none_p_kernel(
         for t in range(PACK):
             gap = sb.tile([P, 2, S], F32, name="gap%d" % t)
             rise = sb.tile([P, 2, S], F32, name="rise%d" % t)
-            make_gate(t)
+            if t < 2:
+                make_gate(2 * t)
+                make_gate(2 * t + 1)
             for lo, hi in ((0, HALF), (HALF, S)) if t == PACK - 1 else ((0, S),):
                 nc.vector.tensor_tensor(
                     out=gap[:, 0, lo:hi], in0=nd_rows[t][:].indirect(entries(l_n2, lo, hi)),
@@ -206,61 +201,55 @@ def tile_picked_triomaxbjointbbig_none_p_kernel(
                 )
                 nc.scalar.activation(out=rise[:, :, lo:hi], in_=gap[:, :, lo:hi], func=ACT.Relu, scale=-1.0)
                 for jb in range(lo // P, hi // P):
-                    for k in range(2):
+                    for term in range(2):
                         nc.tensor.matmul(
-                            mix[t // 2, jb // 2][:, jb % 2, t % 2, :], rise[:, k, jb * P : (jb + 1) * P], ident[:],
-                            start=False, stop=(t % 2 == 1 and jb % 2 == 1 and k == 1), is_transpose=True,
+                            mix[t // 2, jb // 2][:, jb % 2, t % 2, :], rise[:, term, jb * P : (jb + 1) * P], ident[:],
+                            start=False, stop=(t % 2 == 1 and jb % 2 == 1 and term == 1), is_transpose=True,
                         )
 
-        z_turned = {}
+        z_pairs = {}
         z_codes = sb.tile([P, S], U32, name="z_codes", align_bytes=64)
         z_scales = sb.tile([P, S], U8, name="z_scales", align_bytes=64)
 
-        def mix_times_gate(u, jp, b0, b1):
-            tile = sb.tile([P, b1 - b0, P, 2], BF16, name="z_turned_%d_%d_%d" % (u, jp, b0))
+        def mix_times_gate(u, jb0, jb1):
+            jp, s0, s1 = jb0 // 2, jb0 % 2, jb0 % 2 + jb1 - jb0
+            tile = sb.tile([P, s1 - s0, P, 2], BF16, name="z_turned_%d_%d" % (u, jb0))
             nc.vector.tensor_tensor(
                 out=tile[:],
-                in0=mix[u, jp][:, b0:b1].rearrange("j b e p -> j b p e"),
-                in1=gate[jp][:, u, b0:b1],
+                in0=mix[u, jp][:, s0:s1].rearrange("j s e p -> j s p e"),
+                in1=gate[jp][:, u, s0:s1],
                 op=ALU.mult,
             )
-            for b in range(b0, b1):
-                z_turned[u, 2 * jp + b] = tile[:, b - b0].rearrange("j p e -> j (p e)").bitcast(F32)
+            for jb in range(jb0, jb1):
+                z_pairs[u, jb] = tile[:, jb - jb0].rearrange("j p e -> j (p e)").bitcast(F32)
 
-        def turn_back(jb0, jb1, bank):
-            n = jb1 - jb0
-            back = ps.tile([P, n, 2, P], F32, name="back", tag=bank)
+        def quantize_z(jb0, jb1, bank):
+            blocks = jb1 - jb0
+            back = ps.tile([P, blocks, 2, P], F32, name="back", tag=bank)
             for u in range(2):
                 for jb in range(jb0, jb1):
-                    nc.tensor.transpose(back[:, jb - jb0, u, :], z_turned[u, jb], ident[:])
-            rounded = sb.tile([P, n * P * PACK], BF16, name="z_rounded%d" % jb0, align_bytes=64)
+                    nc.tensor.transpose(back[:, jb - jb0, u, :], z_pairs[u, jb], ident[:])
+            rounded = sb.tile([P, blocks * P * PACK], BF16, name="z_rounded%d" % jb0, align_bytes=64)
             nc.scalar.copy(
-                out=rounded[:].bitcast(F32).rearrange("p (b j u) -> p b j u", b=n, u=2),
-                in_=back[:].rearrange("p b u j -> p b j u"),
+                out=rounded[:].bitcast(F32).rearrange("p (s j u) -> p s j u", s=blocks, u=2),
+                in_=back[:].rearrange("p s u j -> p s j u"),
             )
             cols = slice(jb0 * P, jb1 * P)
             nc.vector.quantize_mx(out=z_codes[:, cols].bitcast(FP8X4), scales=z_scales[:, cols], in_=rounded[:])
 
-        mix_times_gate(0, 0, 0, 2)
-        mix_times_gate(0, 1, 0, 2)
-        mix_times_gate(1, 0, 0, 2)
-        mix_times_gate(1, 1, 0, 1)
-        mix_times_gate(1, 1, 1, 2)
-        def quantize_w4(pair, tag):
-            codes = sb.tile([P, HALF], U32, name="q4_codes", tag=tag, align_bytes=64)
-            scales = sb.tile([P, HALF], U8, name="q4_scales%d" % pair, align_bytes=64)
-            in_ = rounded4[:, pair * PACK * HALF : (pair + 1) * PACK * HALF]
-            nc.vector.quantize_mx(out=codes[:].bitcast(FP8X4), scales=scales[:], in_=in_)
-            return codes, scales
-
-        q4 = [quantize_w4(0, "gate1")]
-        turn_back(0, 2, "work0")
-        turn_back(2, 3, "work1")
-        turn_back(3, 4, "mix01")
-        q4.append(quantize_w4(1, "z_rounded3"))
+        pieces = ((0, 2), (2, 3), (3, 4))
+        mix_times_gate(0, 0, 2)
+        mix_times_gate(0, 2, 4)
+        for jb0, jb1 in pieces:
+            mix_times_gate(1, jb0, jb1)
+        q4 = [quantize_weight(rounded4[:, : PACK * HALF], "q4_low", "gate1")]
+        for (jb0, jb1), bank in zip(pieces, ("work0", "work1", "mix01")):
+            quantize_z(jb0, jb1, bank)
+        q4.append(quantize_weight(rounded4[:, PACK * HALF :], "q4_high", "z_rounded3"))
 
         h_rows = b_rows
-        for lo, hi, bank in ((0, 2 * P, "work2"), (2 * P, 3 * P, "mix00"), (3 * P, S, "mix10")):
+        for (jb0, jb1), bank in zip(pieces, ("work2", "mix00", "mix10")):
+            lo, hi = jb0 * P, jb1 * P
             acc = ps.tile([P, hi - lo], F32, name="acc", tag=bank)
             product(acc[:], q4[0], 0, (z_codes[:, lo:hi], z_scales[:, lo:hi]))
             if hi == S:
@@ -273,20 +262,20 @@ def tile_picked_triomaxbjointbbig_none_p_kernel(
             nc.scalar.copy(out=h_rows[t][:, :S], in_=acc[:])
 
         out_rows = out.rearrange("(p t) j -> p t j", t=PACK)
-        looked = {}
+        h_n5 = {}
 
-        def look(t, lo, hi):
-            looked[t, lo] = sb.tile([P, hi - lo], F32, name="looked_%d_%d" % (t, lo))
-            nc.vector.tensor_copy(out=looked[t, lo][:], in_=h_rows[t][:].indirect(entries(l_n5, lo, hi)))
+        def look_up(t, lo, hi):
+            h_n5[t, lo] = sb.tile([P, hi - lo], F32, name="h_n5_%d_%d" % (t, lo))
+            nc.vector.tensor_copy(out=h_n5[t, lo][:], in_=h_rows[t][:].indirect(entries(l_n5, lo, hi)))
 
         def finish(t, lo, hi):
-            res = sb.tile([P, hi - lo], F32, name="res_%d_%d" % (t, lo))
-            nc.vector.tensor_tensor(out=res[:], in0=looked[t, lo][:], in1=h_rows[t][:, lo:hi], op=ALU.max)
-            nc.sync.dma_start(out=out_rows[:, t, lo:hi], in_=res[:])
+            result = sb.tile([P, hi - lo], F32, name="result_%d_%d" % (t, lo))
+            nc.vector.tensor_tensor(out=result[:], in0=h_n5[t, lo][:], in1=h_rows[t][:, lo:hi], op=ALU.max)
+            nc.sync.dma_start(out=out_rows[:, t, lo:hi], in_=result[:])
 
-        steps = [(0, 0, S), (1, 0, S), (2, 0, S), (3, 0, HALF), (3, HALF, S)]
+        steps = [(t, 0, S) for t in range(PACK - 1)] + [(PACK - 1, 0, HALF), (PACK - 1, HALF, S)]
         for i, step in enumerate(steps):
-            look(*step)
+            look_up(*step)
             if i > 0:
                 finish(*steps[i - 1])
         finish(*steps[-1])

from contextlib import ExitStack

import concourse.mybir as mybir
from concourse.masks import make_identity

F32 = mybir.dt.float32
BF16 = mybir.dt.bfloat16
I32 = mybir.dt.int32
U32 = mybir.dt.uint32
U16 = mybir.dt.uint16
U8 = mybir.dt.uint8
FP8X4 = mybir.dt.float8_e4m3fn_x4
ACT = mybir.ActivationFunctionType
ALU = mybir.AluOpType

P = 128
PACK = 4
TOKENS = 2048
S = 512
HALF = S // 2
GROUP = 16
QUADRANT = 32
FLOPS = 4 * 2 * 512 * 512 * 512


def tile_picked_triomaxbjointbbig_none_p_kernel(
    tc, x_words, x_scales, w1, w2, w3, gn, w4, offs, two, three, n1, n2, n3, n4, n5, out
):
    nc = tc.nc
    with ExitStack() as ctx:
        lists = ctx.enter_context(tc.tile_pool(name="lists", bufs=1))
        sb = ctx.enter_context(tc.tile_pool(name="sb", bufs=1))
        ps = ctx.enter_context(tc.psum_pool(name="ps", bufs=1))

        def load_list(src, name):
            tile = lists.tile([P, S // GROUP], U16, name=name)
            nc.sync.dma_start(out=tile[:], in_=src)
            return tile

        def load_columns(src, name, lo, hi):
            tile = sb.tile([P, PACK, hi - lo], F32, name=name, align_bytes=64)
            nc.sync.dma_start(out=tile[:], in_=src.rearrange("(p j) c -> p j c", j=PACK)[:, :, lo:hi])
            return tile

        def entries(tile, lo, hi):
            return tile[:, lo // GROUP : hi // GROUP]

        l_three = load_list(three, "l_three")
        x_bytes = sb.tile([P, TOKENS], U8, name="x_bytes")
        for q in range(P // QUADRANT):
            nc.sync.dma_start(
                out=x_bytes[QUADRANT * q : QUADRANT * (q + 1), :].bitcast(I32),
                in_=x_scales[0, 4 * q : 4 * q + 4, :].bitcast(I32).partition_broadcast(QUADRANT // 4),
            )
        gain = sb.tile([P, PACK], F32, name="gain")
        nc.sync.dma_start(out=gain[:], in_=gn.rearrange("(p t) o -> p (t o)", t=PACK))
        raw3 = [load_columns(w3, "raw3_left", 0, HALF)]
        l_offs = load_list(offs, "l_offs")
        l_two = load_list(two, "l_two")
        raw3.append(load_columns(w3, "raw3_right", HALF, S))
        x_codes = sb.tile([P, TOKENS], U32, name="x_codes")
        nc.sync.dma_start(
            out=x_codes[:].bitcast(I32), in_=x_words[0].rearrange("p n t -> p (n t)").bitcast(I32)
        )
        l_n4 = load_list(n4, "l_n4")
        l_n3 = load_list(n3, "l_n3")
        raw1 = [load_columns(w1, "raw1", 0, S)]
        raw2 = [load_columns(w2, "raw2", 0, S)]
        l_n2 = load_list(n2, "l_n2")
        l_n1 = load_list(n1, "l_n1")
        raw4 = [load_columns(w4, "raw4", 0, S)]
        l_n5 = load_list(n5, "l_n5")

        ident = sb.tile([P, P], F32, name="ident")
        make_identity(nc, ident[:])

        def window(name, tag):
            return sb.tile([P, 2 * S], F32, name=name, tag=tag, align_bytes=64)

        def cleared_window(name):
            tile = window(name, name)
            nc.vector.memset(tile[:, S:], 0.0)
            return tile

        def round_weight(raw, name, pieces):
            rounded = sb.tile([P, PACK * S], BF16, name=name, align_bytes=64)
            dealt = rounded[:].rearrange("p (t m j) -> p m j t", t=PACK, j=PACK)
            step, per_part = P // pieces, P // len(raw)
            for m0 in range(0, P, step):
                part = raw[m0 // per_part][:].rearrange("p j (m t) -> p m j t", t=PACK)
                nc.scalar.copy(out=dealt[:, m0 : m0 + step], in_=part[:, m0 % per_part : m0 % per_part + step])
            return rounded

        def quantize_weight(rounded, name, codes_tag):
            width = rounded.shape[1] // PACK
            codes = sb.tile([P, width], U32, name=name + "_codes", tag=codes_tag, align_bytes=64)
            scales = sb.tile([P, width], U8, name=name + "_scales", align_bytes=64)
            nc.vector.quantize_mx(out=codes[:].bitcast(FP8X4), scales=scales[:], in_=rounded)
            return codes, scales

        def pick(table, token_list, dtype, tag):
            picked = sb.tile([P, S], dtype, name="picked", tag=tag, align_bytes=64)
            nc.vector.tensor_copy(out=picked[:], in_=table[:].indirect(token_list[:]))
            return picked

        def product(acc, weight, block, moving):
            cols = slice(block * P, (block + 1) * P)
            nc.tensor.matmul_mx(
                out=acc,
                lhsT=weight[0][:, cols].bitcast(FP8X4),
                lhsT_scale=weight[1][:, cols],
                rhs=moving[0][:].bitcast(FP8X4),
                rhs_scale=moving[1][:],
                start=True,
                stop=True,
            )

        def project(weight, tokens, t, factor, row, bank):
            acc = ps.tile([P, S], F32, name="acc", tag=bank)
            product(acc[:], weight, t, tokens)
            nc.scalar.activation(out=row[:, :S], in_=acc[:], func=ACT.Copy, scale=factor[:, t : t + 1])

        g_sign = sb.tile([P, PACK], F32, name="g_sign")
        g_abs = sb.tile([P, PACK], F32, name="g_abs")
        g_neg = sb.tile([P, PACK], F32, name="g_neg")
        nc.scalar.activation(out=g_sign[:], in_=gain[:], func=ACT.Sign)
        nc.scalar.activation(out=g_abs[:], in_=gain[:], func=ACT.Abs)
        nc.scalar.activation(out=g_neg[:], in_=g_abs[:], func=ACT.Copy, scale=-1.0)

        bytes3 = pick(x_bytes, l_three, U8, "bytes3")
        bytes1 = pick(x_bytes, l_offs, U8, "bytes1")
        bytes2 = pick(x_bytes, l_two, U8, "bytes2")
        rounded3 = round_weight(raw3, "rounded3", len(raw3))
        q3 = quantize_weight(rounded3[:], "q3", "q3_codes")
        codes3 = pick(x_codes, l_three, U32, "codes3")
        codes1 = pick(x_codes, l_offs, U32, "rounded3")
        codes2 = pick(x_codes, l_two, U32, "codes2")

        b_rows = [cleared_window("b%d" % t) for t in range(PACK)]
        y1_row = cleared_window("y1")
        for t in range(PACK):
            project(q3, (codes3, bytes3), t, g_sign, b_rows[t], "work%d" % t)
        rounded1 = round_weight(raw1, "rounded1", 4)
        rounded2 = round_weight(raw2, "rounded2", 2)
        q1 = quantize_weight(rounded1[:], "q1", "q1_codes")
        q2 = quantize_weight(rounded2[:], "q2", "q2_codes")
        y_rows = [window("y0", "y0"), y1_row, window("y2", "y2"), window("y3", "rounded1")]
        nd_rows = [window("nd0", "raw1"), window("nd1", "rounded2"), window("nd2", "raw2"), window("nd3", "nd3")]
        for t in range(PACK):
            project(q1, (codes1, bytes1), t, g_abs, y_rows[t], "work%d" % (2 * t % 4))
            project(q2, (codes2, bytes2), t, g_neg, nd_rows[t], "work%d" % ((2 * t + 1) % 4))
        rounded4 = round_weight(raw4, "rounded4", 4)

        b_n4 = [rows[:, S:] for rows in (y_rows[0], nd_rows[3], y_rows[2], y_rows[3])]
        diff = [rows[:, S:] for rows in nd_rows]
        for t in range(PACK):
            nc.vector.tensor_copy(out=b_n4[t], in_=b_rows[t][:].indirect(l_n4[:]))
        for t in range(PACK):
            nc.vector.tensor_tensor(out=diff[t], in0=b_rows[t][:].indirect(l_n3[:]), in1=b_n4[t], op=ALU.subtract)

        mix = {}
        for u in range(2):
            for jp in range(2):
                bank = ps.tile([P, 2, 2, P], F32, name="mix", tag="mix%d%d" % (u, jp))
                for e in range(2):
                    for term, rows in enumerate((y_rows, nd_rows)):
                        for s in range(2):
                            jb = 2 * jp + s
                            nc.tensor.matmul(
                                bank[:, s, e, :], rows[2 * u + e][:, jb * P : (jb + 1) * P], ident[:],
                                start=(e == 0 and term == 0 and s == 0), stop=False, is_transpose=True,
                            )
                mix[u, jp] = bank

        gate = [sb.tile([P, 2, 2, P, 2], F32, name="gate%d" % jp, align_bytes=64) for jp in range(2)]

        def make_gate(jb):
            turned = ps.tile([P, PACK, P], F32, name="turned", tag=("work3", "work1")[jb % 2])
            for t in range(PACK):
                nc.tensor.transpose(turned[:, t, :], diff[t][:, jb * P : (jb + 1) * P], ident[:])
            nc.scalar.activation(
                out=gate[jb // 2][:, :, jb % 2, :, :],
                in_=turned[:].rearrange("j (u e) p -> j u p e", e=2),
                func=ACT.Tanh,
            )

        for t in range(PACK):
            gap = sb.tile([P, 2, S], F32, name="gap%d" % t)
            rise = sb.tile([P, 2, S], F32, name="rise%d" % t)
            if t < 2:
                make_gate(2 * t)
                make_gate(2 * t + 1)
            for lo, hi in ((0, HALF), (HALF, S)) if t == PACK - 1 else ((0, S),):
                nc.vector.tensor_tensor(
                    out=gap[:, 0, lo:hi], in0=nd_rows[t][:].indirect(entries(l_n2, lo, hi)),
                    in1=y_rows[t][:, lo:hi], op=ALU.add,
                )
                nc.vector.tensor_tensor(
                    out=gap[:, 1, lo:hi], in0=y_rows[t][:].indirect(entries(l_n1, lo, hi)),
                    in1=nd_rows[t][:, lo:hi], op=ALU.add,
                )
                nc.scalar.activation(out=rise[:, :, lo:hi], in_=gap[:, :, lo:hi], func=ACT.Relu, scale=-1.0)
                for jb in range(lo // P, hi // P):
                    for term in range(2):
                        nc.tensor.matmul(
                            mix[t // 2, jb // 2][:, jb % 2, t % 2, :], rise[:, term, jb * P : (jb + 1) * P], ident[:],
                            start=False, stop=(t % 2 == 1 and jb % 2 == 1 and term == 1), is_transpose=True,
                        )

        z_pairs = {}
        z_codes = sb.tile([P, S], U32, name="z_codes", align_bytes=64)
        z_scales = sb.tile([P, S], U8, name="z_scales", align_bytes=64)

        def mix_times_gate(u, jb0, jb1):
            jp, s0, s1 = jb0 // 2, jb0 % 2, jb0 % 2 + jb1 - jb0
            tile = sb.tile([P, s1 - s0, P, 2], BF16, name="z_turned_%d_%d" % (u, jb0))
            nc.vector.tensor_tensor(
                out=tile[:],
                in0=mix[u, jp][:, s0:s1].rearrange("j s e p -> j s p e"),
                in1=gate[jp][:, u, s0:s1],
                op=ALU.mult,
            )
            for jb in range(jb0, jb1):
                z_pairs[u, jb] = tile[:, jb - jb0].rearrange("j p e -> j (p e)").bitcast(F32)

        def quantize_z(jb0, jb1, bank):
            blocks = jb1 - jb0
            back = ps.tile([P, blocks, 2, P], F32, name="back", tag=bank)
            for u in range(2):
                for jb in range(jb0, jb1):
                    nc.tensor.transpose(back[:, jb - jb0, u, :], z_pairs[u, jb], ident[:])
            rounded = sb.tile([P, blocks * P * PACK], BF16, name="z_rounded%d" % jb0, align_bytes=64)
            nc.scalar.copy(
                out=rounded[:].bitcast(F32).rearrange("p (s j u) -> p s j u", s=blocks, u=2),
                in_=back[:].rearrange("p s u j -> p s j u"),
            )
            cols = slice(jb0 * P, jb1 * P)
            nc.vector.quantize_mx(out=z_codes[:, cols].bitcast(FP8X4), scales=z_scales[:, cols], in_=rounded[:])

        pieces = ((0, 2), (2, 3), (3, 4))
        mix_times_gate(0, 0, 2)
        mix_times_gate(0, 2, 4)
        for jb0, jb1 in pieces:
            mix_times_gate(1, jb0, jb1)
        q4 = [quantize_weight(rounded4[:, : PACK * HALF], "q4_low", "gate1")]
        for (jb0, jb1), bank in zip(pieces, ("work0", "work1", "mix01")):
            quantize_z(jb0, jb1, bank)
        q4.append(quantize_weight(rounded4[:, PACK * HALF :], "q4_high", "z_rounded3"))

        h_rows = b_rows
        for (jb0, jb1), bank in zip(pieces, ("work2", "mix00", "mix10")):
            lo, hi = jb0 * P, jb1 * P
            acc = ps.tile([P, hi - lo], F32, name="acc", tag=bank)
            product(acc[:], q4[0], 0, (z_codes[:, lo:hi], z_scales[:, lo:hi]))
            if hi == S:
                nc.vector.tensor_copy(out=h_rows[0][:, lo:hi], in_=acc[:])
            else:
                nc.scalar.copy(out=h_rows[0][:, lo:hi], in_=acc[:])
        for t, bank in ((1, "work3"), (2, "work0"), (3, "mix11")):
            acc = ps.tile([P, S], F32, name="acc", tag=bank)
            product(acc[:], q4[t // 2], t % 2, (z_codes, z_scales))
            nc.scalar.copy(out=h_rows[t][:, :S], in_=acc[:])

        out_rows = out.rearrange("(p t) j -> p t j", t=PACK)
        h_n5 = {}

        def look_up(t, lo, hi):
            h_n5[t, lo] = sb.tile([P, hi - lo], F32, name="h_n5_%d_%d" % (t, lo))
            nc.vector.tensor_copy(out=h_n5[t, lo][:], in_=h_rows[t][:].indirect(entries(l_n5, lo, hi)))

        def finish(t, lo, hi):
            result = sb.tile([P, hi - lo], F32, name="result_%d_%d" % (t, lo))
            nc.vector.tensor_tensor(out=result[:], in0=h_n5[t, lo][:], in1=h_rows[t][:, lo:hi], op=ALU.max)
            nc.sync.dma_start(out=out_rows[:, t, lo:hi], in_=result[:])

        steps = [(t, 0, S) for t in range(PACK - 1)] + [(PACK - 1, 0, HALF), (PACK - 1, HALF, S)]
        for i, step in enumerate(steps):
            look_up(*step)
            if i > 0:
                finish(*steps[i - 1])
        finish(*steps[-1])
